import numpy as np, ml_dtypes
CORES = [25,29,65,69,153,157,193,197]
N = 8
BF = ml_dtypes.bfloat16
W, U, SH, B, T, DEL, LIM = 2560, 320, 3, 256, 8, 3, 16
def parts(rng):
    return (rng.integers(0, 64, (N, 8, 16, W)), rng.integers(0, W, (N, 8, 16, U)), rng.integers(0, W, (N, 8, 16, B)), rng.integers(0, W, (N, 8, B)), rng.integers(0, 64, (N, 8, 16, B)))
def pack(x, canal, trail, cut, z):
    return {"x": x.reshape(N, 128, W).astype(np.float32).astype(BF), "canal": np.ascontiguousarray(canal.reshape(N, 128, U)).astype(np.int32), "trail": np.ascontiguousarray(trail.reshape(N, 128, B)).astype(np.int32),
            "cut": np.ascontiguousarray(cut).astype(np.int32), "z": z.reshape(N, 128, B).astype(np.float32).astype(BF)}
def setup_inputs(rng):
    return pack(*parts(rng))
def setup_inputs_spread(rng):
    def low(*shape): return np.minimum((W * rng.random(shape) ** 3).astype(np.int64), W - 1)
    def size(n): return np.minimum((64.0 ** rng.random((N, 8, 1, n)) * rng.random((N, 8, 16, n))).astype(np.int64), 63)
    return pack(size(W), low(N, 8, 16, U), low(N, 8, 16, B), low(N, 8, B), size(B))
def tips(rng, *shape):
    q = rng.random(shape)
    return np.where(q < 0.36, 0, np.where(q < 0.72, W - 1, rng.integers(0, W, shape)))
def setup_inputs_ends(rng):
    k = rng.random((N, 8, 1, W)); x = np.where(k < 0.2, 0, np.where(k < 0.4, 63, 63 * rng.integers(0, 2, (N, 8, 16, W))))
    one = (np.arange(16).reshape(1, 1, 16, 1) == rng.integers(0, 16, (N, 8, 1, W))) & (rng.random((N, 8, 1, W)) < 0.15)
    x = np.where(one, np.where(x == 63, 62, 1), x)
    for q in (1, N - 1): x[q] = np.where(rng.random((8, 1, W)) < 0.3, 32 + LIM + rng.integers(0, 3, (8, 1, W)), x[q])
    k = rng.random((N, 8, 1, B)); z = np.where(k < 0.3, 0, np.where(k < 0.45, 63, 63 * rng.integers(0, 2, (N, 8, 16, B))))
    for q in (0, 1, N - 1): z[q] = np.repeat(63 * rng.integers(0, 2, (8, 1, B)), 16, axis=1)
    z[:, :, :, B - 1] = 0
    canal, trail, cut = tips(rng, N, 8, 16, U), tips(rng, N, 8, 16, B), tips(rng, N, 8, B); cut[:, :, B - 1] = W - 1
    for r in range(N):
        for g in range(8):
            a = 2 * int(rng.integers(W // 8, W // 4)); b = a - 1; rows = rng.permutation(15)[:2]
            x[r, g, :, 0] = 0 if r in (0, 1, N - 1) else 63 * ((r + g) % 2)
            x[r, g, :, W - 1] = 63; x[r, g, :, a] = 63; x[r, g, :, b] = 63; x[r, g, int(rng.integers(0, 16)), b] = 62
            canal[r, g, :, U - 1] = W - 1; canal[r, g, rows[0], U - 1] = a; canal[r, g, rows[1], U - 1] = b
    w = 16 - DEL
    for q in (1, N - 1): trail[q, :, w] = np.where(z[q, :, 0] == 0, W - 1, 0)
    trail[1, 0, w, 0] = W - 1 - trail[1, 0, w, 0]
    trail[0, :, w] = np.where(z[0, :, 0] == 0, 0, W - 1)
    for q in range(2, N - 1):
        trail[q, 7, w] = np.where((trail[q, 7, w] >> SH) == U - 1, 0, trail[q, 7, w]); trail[q, 7, w, B - 1] = W - 1
    return pack(x, canal, trail, cut, z)
def setup_inputs_corners(rng):
    x, canal, trail, cut, z = parts(rng); s = int(rng.integers(0, 8)); H = 1 << SH
    for r in range(N):
        for g in range(8):
            kind = (r + g + s) % 8
            if kind == 0: cut[r, g] = (0, W - 1, int(rng.integers(0, W)))[r % 3]
            if kind == 1:
                u = rng.integers(0, U, (16, 1)); u[16 - DEL] = U - 1; u[17 - DEL if DEL > 1 else 0] = 0
                trail[r, g] = (u << SH) + rng.integers(0, H, (16, B))
            if kind == 2: trail[r, g] = (np.argsort(rng.random((16, U)), axis=1)[:, :B] << SH) + rng.integers(0, H, (16, B))
            if kind == 3:
                canal[r, g] = (np.arange(U)[None, :] << SH) + rng.integers(0, H, (16, U))
                cut[r, g] = rng.permutation(W)[:B]; trail[r, g] = cut[r, g][None, :]
            if kind == 4: x[r, g] = 30 + rng.integers(0, 4, (16, W)); z[r, g] = 30 + rng.integers(0, 4, (16, B))
            if kind == 5: x[r, g] = rng.integers(0, 4, (16, W)); z[r, g] = rng.integers(60, 64, (16, B))
            if kind == 6:
                at = np.argsort(rng.random((16, W)), axis=0); n = rng.integers(8, 10, (1, W)); sg = 2 * rng.integers(0, 2, (16, W)) - 1
                x[r, g] = 24 + sg * np.where(at < n, LIM + 1, LIM); z[r, g] = 24
            if kind == 7:
                x[r, g] = rng.integers(60, 64, (16, 4))[:, rng.integers(0, 4, W)]
                canal[r, g] = -np.sort(-canal[r, g], axis=0); canal[r, g, :, ::5] = canal[r, g, :1, ::5]
    return pack(x, canal, trail, cut, z)
def setup_inputs_full(rng):
    x, canal, trail, cut, z = parts(rng); w = 16 - DEL; w1 = (17 - DEL) % 16; H = 1 << SH; q = B // 4
    for r in range(N):
        for g in range(8):
            v = rng.integers(0, 64, W); y = np.full(B, 16); l = canal[r, g]; h = trail[r, g]
            if r == 0:
                h[w] = (rng.permutation(U)[:B] << SH) + rng.integers(0, H, B); v[h[w]] = rng.integers(40, 59, B)
            elif r == 1:
                o = rng.permutation(W - H); best = o[:B]; low = o[B:]
                v = rng.integers(0, 21, W); v[best] = rng.integers(25, 33, B)
                u = rng.permutation(U)[:B]; cut[r, g] = (u << SH) + rng.integers(0, H, B)
                l[:] = low[rng.integers(0, len(low), (16, U))]; l[rng.integers(0, 16, B), u] = best
                h[:] = rng.integers(0, W - H, (16, B))
                h[w, :B - 1] = (rng.permutation(U - 1)[:B - 1] << SH) + rng.integers(0, H, B - 1); h[w, B - 1] = W - 1
            elif r == 2:
                a = np.flatnonzero((v >= 16) & (v <= 32)); h[w] = a[rng.integers(0, len(a), B)]; h[w1] = a[rng.integers(0, len(a), B)]
                if g in (0, 3, 7):
                    far = np.flatnonzero(v >= 40); i = 0 if g == 0 else B - 1 if g == 7 else int(rng.integers(0, B))
                    h[w, i] = far[int(rng.integers(0, len(far)))]
            else:
                v = rng.integers(0, 63, W); v[0] = 63; v[W - 1] = 63
                y = rng.integers(0, 64, B); i = rng.permutation(B); u = rng.permutation(U - 1)[:2 * q]
                y[i[:q]] = 63; y[i[q:2 * q]] = 0; cut[r, g, i[:2 * q]] = (u << SH) + rng.integers(0, H, 2 * q)
                l[:, u[:q]] = W - 1; l[:, u[q:]] = rng.integers(1, W - 1, (16, q))
                l[rng.integers(0, 2, q), u[q:]] = 0; l[rng.integers(13, 16, q), u[q:]] = W - 1
            x[r, g] = v; z[r, g] = y
            if r > 2: x[r, g, int(rng.integers(0, 16)), 0] = 62
    return pack(x, canal, trail, cut, z)
def setup_inputs_meet(rng):
    x, canal, trail, cut, z = parts(rng)
    for r in range(N):
        for g in range(8):
            s = rng.permutation(W)[:64]; s[0] = W - 1
            canal[r, g] = s[rng.integers(0, 64, (16, U))]; trail[r, g] = s[rng.integers(0, 64, (16, B))]; cut[r, g] = s[rng.integers(0, 64, B)]
    return pack(x, canal, trail, cut, z)
def check_inputs(d):
    bad = []
    for k, hi in (("x", 63), ("canal", W - 1), ("trail", W - 1), ("cut", W - 1), ("z", 63)):
        a = np.asarray(d[k]).astype(np.float64)
        if not (np.min(a) >= 0 and np.max(a) <= hi): bad.append("range of " + k)
        if not np.all(a == np.floor(a)): bad.append("whole numbers in " + k)
    return bad
def reference(x, canal, trail, cut, z):
    X = x.astype(np.float32).astype(np.int64).reshape(N, 8, 16, W); C = canal.astype(np.int64).reshape(N, 8, 16, U); G = trail.astype(np.int64).reshape(N, 8, 16, B)
    V = cut.astype(np.int64).reshape(N, 8, B); Z = z.astype(np.float32).astype(np.int64).reshape(N, 8, 16, B); skips = np.zeros(N, np.int64)
    for t in range(T):
        lim = LIM + (skips & 3); skips = np.zeros(N, np.int64); come = np.zeros_like(Z); row = (t + 16 - DEL) % 16
        for r in range(N):
            for g in range(8):
                a, l, h, q = X[r, g], C[r, g], G[r, g], Z[r, g]
                k = l[:, V[r, g] >> SH]
                score = np.add.reduce(np.maximum(a[:, k] - q[:, None, :], 0), axis=0)
                c = np.min(np.where(score == np.max(score, axis=0), k, W), axis=0)
                cut_off = np.sum(np.abs(a[:, h] - q[:, None, :]) > lim[r], axis=0) >= 9
                w = h[row] + 0; skip = cut_off[row]; xw = a[:, w]; xc = a[:, c]
                first = np.zeros(B, bool); first[np.unique(w >> SH, return_index=True)[1]] = True
                new = np.where(skip, np.minimum(xw + 4, 63), (xw + q) >> 1)
                a[:, w[first]] = new[:, first]
                m = first & ~skip; u = w[m] >> SH
                l[:, u] = np.where(cut_off[:, m], l[:, u], h[:, m])
                h[:] = np.where(cut_off, k, h); h[t] = c
                a[:, c] = xc >> 1
                V[r, g] = c; skips[r] += np.sum(skip)
                come[(r + 1 + t % (N - 1)) % N, g] = (q + xc) >> 1
        Z = come
    return {"yx": X.reshape(N, 128, W).astype(np.float32).astype(BF), "yl": C.reshape(N, 128, U).astype(np.float32), "yg": G.reshape(N, 128, B).astype(np.float32)}

import math
from concourse.mybir import AluOpType as OP, ActivationFunctionType as AF

NC, NU, B, STEPS, CEN = 2560, 320, 256, 8, 1280
BIG = 4096.0
LN = math.log(1.75)
BY_ACT = (0, 1, 2)
ORDER = "AABBBABA"
NET = 7.0
PEC = 0.0006
SMALL = 0.3
GAT, SCA, CY = 1.5, 3.0, 0.001
BK = {"zn": "b0", "dup": "b1", "skip": "b6"}

BUFS = {
    "bfloat16": "xs 2816 xraw 2560 zraw 256 zland 1792 zn 1792 relay 1792 zr 2048 D 4096 AB 4096 SG 4096 E 4096 R 4096 SM 256 NM 256 SW 256 "
                "NW 256 PB 256 XM 256 XW 256 xc 256 xh 256 EQ 240 G12 512 LOH 576 Fs 160 Pf 256 skb 16 W 144 Ib 128 Ihalf 128 Ineg 128 "
                "Im1 128 BD 128 one 128 four 256 TRI 240 T12 640 R2 160 xo 2560",
    "float16": "can16 320 tr16 256 cut16 256 GV 1024 KN 512 TRK 1024 c16 16 Ih 128 Imh 128 Y 144 X 512 Xs 512 PS 256 ZW 144 trO 256 uh 16 hh 16 vh 16",
    "float32": "can 576 BS 512 VN 256 kS 128 k1 128 k2 64 k3 32 km 16 kd 16 cF 16 dd 16 wuF 64 ssj 16 sc 1 lc 2 M2 32 M3 32 M4 32 ioF 320 "
               "pc 24 tF 320 tG 320 tH 320 DUMP 32 iL 16 THR 16 swa 2 swt 2 outF 320 outG 256",
    "int32": "canI 320 trI 256 cutI 256 kr 16 cdI 16 scI 1 sdI 1 ioI 320 pI 1 qI 4 tI 320 tI2 320",
    "uint16": "GL 512 KL 256 cl 16 vuL 96 cdl 32 hl 16 wcl 32",
}
SCRATCH = {"b%d" % i: ("psum", [128, 512], "float32") for i in range(8)}
for _dt, _s in BUFS.items():
    _l = _s.split()
    for _i in range(0, len(_l), 2):
        SCRATCH[_l[_i]] = ("sbuf", [128, int(_l[_i + 1])], _dt)
SEMAPHORES = ["sv", "sa", "sp", "sg", "zl"] + ["z%d" % t for t in range(7)] + ["r%d" % t for t in range(7)] + ["d%d" % i for i in range(9)]


def col(i):
    return ("pc", i, i + 1, 1)


def c(name, lo, hi, st=1):
    return (name, lo, hi, st)


def ap(T, a):
    t = T[a[0]]
    if len(a) == 5:
        return t[0:a[4], a[1]:a[2]:a[3]] if a[3] > 1 else t[0:a[4], a[1]:a[2]]
    return t[:, a[1]:a[2]:a[3]] if a[3] > 1 else t[:, a[1]:a[2]]


def width(a):
    return (a[2] - a[1] + a[3] - 1) // a[3]


def half(a):
    return SCRATCH[a[0]][2] in ("bfloat16", "float16", "uint16")


def add(p, q, fn, reads, writes, cost, dsem=None, tag=""):
    i = len(p["ops"])
    deps = {}
    for lst, wr in ((reads, False), (writes, True)):
        for a in lst:
            name, lo, hi, st = a[:4]
            psum = SCRATCH[name][0] == "psum"
            keep = []
            for e in p["acc"].setdefault(name, []):
                j, l2, h2, s2, w2 = e
                qj = p["ops"][j]["q"] if j < i else q
                apart = h2 <= lo or hi <= l2 or (st == s2 and (lo - l2) % st)
                conf = j < i and ((not apart and (wr or w2)) or (psum and qj != q))
                if conf:
                    deps[j] = deps.get(j, False) or qj != q or q != "p"
                if not (conf and wr and lo <= l2 and h2 <= hi and st in (1, s2) and (not psum or qj == q)):
                    keep.append(e)
            keep.append((i, lo, hi, st, wr))
            p["acc"][name] = keep
    p["ops"].append({"q": q, "fn": fn, "deps": deps, "cost": cost, "ext": None, "dsem": dsem, "tag": tag})
    return i


def ts(p, out, in0, s1, op0, s2=None, op1=None, tag=""):
    def fn(g, T):
        a1 = ap(T, s1) if isinstance(s1, tuple) else s1
        a2 = ap(T, s2) if isinstance(s2, tuple) else s2
        if op1 is None:
            return g.vector.tensor_scalar(ap(T, out), ap(T, in0), a1, None, op0)
        return g.vector.tensor_scalar(ap(T, out), ap(T, in0), a1, a2, op0, op1)
    f = 0.5 if half(out) and half(in0) else 1.0
    return add(p, "v", fn, [in0] + [s for s in (s1, s2) if isinstance(s, tuple)], [out], 0.01 + max(64, width(out) * f) * CY, tag=tag)


def tt(p, out, in0, in1, op, tag=""):
    f = 1 if SCRATCH[in0[0]][0] == "psum" or SCRATCH[in1[0]][0] == "psum" else 2
    return add(p, "v", lambda g, T: g.vector.tensor_tensor(ap(T, out), ap(T, in0), ap(T, in1), op), [in0, in1], [out], 0.01 + max(64, width(out) * f) * CY, tag=tag)


def cp(p, out, in0, tag=""):
    f = 0.5 if half(out) and half(in0) else 1.0
    return add(p, "v", lambda g, T: g.vector.tensor_copy(ap(T, out), ap(T, in0)), [in0], [out], 0.01 + max(64, width(out) * f) * CY, tag=tag)


def memset(p, out, val):
    return add(p, "v", lambda g, T: g.vector.memset(ap(T, out), val), [], [out], 0.01 + max(64, width(out)) * CY)


def gtt(p, out, win, offs, in1, op, tag=""):
    return add(p, "v", lambda g, T: g.vector.tensor_tensor(ap(T, out), ap(T, win).indirect(ap(T, offs)), ap(T, in1), op), [win, offs, in1], [out], 0.05 + width(out) * GAT * CY, tag=tag)


def gcp(p, out, win, offs, tag=""):
    return add(p, "v", lambda g, T: g.vector.tensor_copy(ap(T, out), ap(T, win).indirect(ap(T, offs))), [win, offs], [out], 0.05 + width(out) * GAT * CY, tag=tag)


def scat(p, win, offs, in0, tag=""):
    return add(p, "v", lambda g, T: g.vector.tensor_copy(ap(T, win).indirect(ap(T, offs)), ap(T, in0)), [offs, in0], [win], 0.05 + width(in0) * SCA * CY, tag=tag)


def vtr(p, out, in0, tag=""):
    return add(p, "v", lambda g, T: g.vector.transpose(ap(T, out), ap(T, in0)), [in0], [out], 0.01 + 64 * CY, tag=tag)


def act(p, out, in0, func, bias=None, scale=None, accum=None, offs=None, tag=""):
    def fn(g, T):
        kw = {}
        if bias is not None:
            kw["bias"] = ap(T, bias) if isinstance(bias, tuple) else bias
        if scale is not None:
            kw["scale"] = ap(T, scale) if isinstance(scale, tuple) else scale
        if accum is not None:
            kw["accum_out"] = ap(T, accum)
        src = ap(T, in0) if offs is None else ap(T, in0).indirect(ap(T, offs))
        return g.scalar.activation(ap(T, out), src, func, **kw)
    return add(p, "a", fn, [in0] + [s for s in (bias, scale, offs) if isinstance(s, tuple)], [out] + ([accum] if accum else []), 0.065 + width(out) * (GAT if offs else 1.0) * CY, tag=tag)


def mm(p, out, lhsT, rhs, start, stop):
    i = add(p, "p", lambda g, T: g.tensor.matmul(ap(T, out), ap(T, lhsT), ap(T, rhs), start, stop), [lhsT, rhs], [out], max(min(64, width(lhsT)), width(out)) * PEC)
    if out[0] in p["bank"]:
        p["ops"][i]["deps"].setdefault(p["bank"][out[0]], False)
    p["bank"][out[0]] = i
    return i


def iota(p, out, pattern, base, chan):
    return add(p, "g", lambda g, T: g.iota(ap(T, out), pattern, base, chan), [], [out], 0.13 + width(out) * 2 * CY)


def dma(p, out, in0, k, lo=None, hi=None):
    def fn(g, T):
        o = ap(T, out) if isinstance(out, tuple) else T[out][:] if lo is None else T[out][:, lo:hi]
        i = ap(T, in0) if isinstance(in0, tuple) else T[in0][:] if lo is None else T[in0][:, lo:hi]
        return g.sync.dma_start(o, i)
    return add(p, "sync", fn, [a for a in (in0,) if isinstance(a, tuple)], [a for a in (out,) if isinstance(a, tuple)], 2.5, dsem="d%d" % k)


P_, PM, PG, W0, P16, M0, M1, M2C, M0X2, NM1, C20, DC, MB0, MB1, TG, PP, PI, TMP, PZ = range(19)


def constants(p):
    iota(p, c("pI", 0, 1), [[1, 1]], 0, 1)
    iota(p, c("ioI", 0, 320), [[1, 320]], 0, 0)
    ts(p, c("qI", 0, 1), c("pI", 0, 1), 15, OP.bitwise_and)
    ts(p, c("qI", 1, 2), c("pI", 0, 1), 4, OP.logical_shift_right)
    ts(p, c("qI", 2, 3), c("qI", 1, 2), 1, OP.bitwise_and)
    cp(p, col(P_), c("pI", 0, 1))
    cp(p, col(PM), c("qI", 0, 1))
    cp(p, col(PG), c("qI", 1, 2))
    cp(p, col(MB1), c("qI", 2, 3))
    ts(p, col(MB0), col(MB1), -1.0, OP.mult, 1.0, OP.add)
    ts(p, col(W0), col(PG), 16.0, OP.mult, 15.0, OP.add)
    ts(p, col(P16), col(P_), 16.0, OP.add)
    for k, dst in ((0, M0), (1, M1), (2, M2C)):
        ts(p, col(dst), col(PM), float(k), OP.is_equal)
    ts(p, col(M0X2), col(M0), 2.0, OP.mult)
    ts(p, col(NM1), col(M1), -1.0, OP.mult)
    ts(p, col(C20), col(PG), 20.0, OP.mult)
    ts(p, col(DC), col(PM), float(NC), OP.add)
    ts(p, col(PZ), col(P_), 16.0, OP.mult, 15.0, OP.add)
    cp(p, c("ioF", 0, 320), c("ioI", 0, 320))
    io, io144 = c("ioF", 0, 128), c("ioF", 0, 144)
    ts(p, col(TMP), col(PM), 13.0, OP.is_ge, -16.0, OP.mult)
    ts(p, col(PP), col(P_), col(TMP), OP.add, 3.0, OP.add)
    ts(p, col(TMP), col(PM), 3.0, OP.is_lt, 16.0, OP.mult)
    ts(p, col(PI), col(P_), col(TMP), OP.add, -3.0, OP.add)
    ts(p, c("PS", 0, 128), io, col(PP), OP.is_equal)
    ts(p, c("PS", 128, 256), io, col(PI), OP.is_equal)
    for s in (0, 1):
        for d in (0, 1):
            ts(p, col(TG), col(P_), 16.0 * (d - s) + 1.0, OP.add, col(MB1 if s else MB0), OP.mult)
            ts(p, col(TMP), col(TG), -1.0, OP.add)
            k = 128 * (2 * s + d)
            ts(p, c("X", k, k + 128), io, col(TMP), OP.is_equal)
    ts(p, c("Xs", 0, 512), c("X", 0, 512), -1.0 / 4096.0, OP.mult)
    ts(p, c("ZW", 0, 144), io144, col(PZ), OP.is_equal)
    ts(p, c("Ih", 0, 128), io, col(P_), OP.is_equal)
    ts(p, c("Imh", 0, 128), io, col(P_), OP.is_equal, -1.0, OP.mult)
    ts(p, c("W", 0, 144), io144, col(W0), OP.is_equal)
    ts(p, c("Ib", 0, 128), io, col(P_), OP.is_equal)
    act(p, c("Ihalf", 0, 128), c("Ib", 0, 128), AF.Copy, scale=0.5)
    act(p, c("Ineg", 0, 128), c("Ib", 0, 128), AF.Copy, scale=-BIG)
    act(p, c("Im1", 0, 128), c("Ib", 0, 128), AF.Copy, scale=-1.0)
    ts(p, c("Y", 0, 144), io144, col(P16), OP.is_equal)
    ts(p, c("tI", 0, 320), c("ioI", 0, 320), 4, OP.logical_shift_right)
    ts(p, c("tI2", 0, 320), c("ioI", 0, 320), 15, OP.bitwise_and)
    ts(p, c("BD", 0, 128), c("tI", 0, 128), col(PG), OP.is_equal)
    ts(p, c("T12", 0, 320), c("tI2", 0, 320), col(PM), OP.is_equal)
    ts(p, c("tF", 0, 320), c("tI", 0, 320), -10.0, OP.add)
    tt(p, c("tG", 0, 320), c("tF", 0, 320), c("tF", 0, 320), OP.mult)
    ts(p, c("tG", 0, 320), c("tG", 0, 320), col(M1), OP.mult, col(M2C), OP.add)
    ts(p, c("tF", 0, 320), c("tF", 0, 320), col(M0), OP.mult)
    tt(p, c("T12", 320, 640), c("tF", 0, 320), c("tG", 0, 320), OP.add)
    iota(p, c("tI", 0, 160), [[0, 8], [1, 20]], -10, 0)
    iota(p, c("tI2", 0, 160), [[1, 8], [0, 20]], 0, 0)
    cp(p, c("tH", 0, 160), c("tI", 0, 160))
    tt(p, c("tG", 0, 160), c("tH", 0, 160), c("tH", 0, 160), OP.mult)
    ts(p, c("tF", 0, 160), c("tH", 0, 160), col(M0X2), OP.mult, col(NM1), OP.add)
    ts(p, c("tG", 0, 160), c("tG", 0, 160), -1.0, OP.mult, 1.0, OP.add)
    ts(p, c("tG", 0, 160), c("tG", 0, 160), col(M2C), OP.mult)
    tt(p, c("tF", 0, 160), c("tF", 0, 160), c("tG", 0, 160), OP.add)
    ts(p, c("tG", 0, 160), c("tI2", 0, 160), col(PG), OP.is_equal)
    tt(p, c("R2", 0, 160), c("tF", 0, 160), c("tG", 0, 160), OP.mult)
    iota(p, c("tI", 0, 240), [[1, 15], [0, 16]], 1, 0)
    ts(p, c("TRI", 0, 240), c("tI", 0, 240), col(PM), OP.is_gt, 8192.0, OP.mult)
    iota(p, c("tI2", 0, 16), [[16, 16]], 0, 0)
    ts(p, c("iL", 0, 16), c("tI2", 0, 16), col(PM), OP.add)
    ts(p, c("DUMP", 0, 16), c("iL", 0, 16), float(NC), OP.add)
    ts(p, c("DUMP", 16, 32), c("iL", 0, 16), float(NU), OP.add)
    ts(p, c("iL", 0, 16), c("iL", 0, 16), -LN, OP.mult, 128 * LN + math.log(2.5), OP.add)
    act(p, c("THR", 0, 16), c("iL", 0, 16), AF.Exp)
    for h in (0, 1):
        ts(p, c("swa", h, h + 1), col(P_), -0.5 * LN, OP.mult, 0.5 * LN * (128 - 128 * h), OP.add)
    act(p, c("swt", 0, 2), c("swa", 0, 2), AF.Exp)
    memset(p, c("one", 0, 128), 1.0)
    memset(p, c("four", 0, 256), 4.0)
    memset(p, c("lc", 0, 1), -16.5)


def X(s, d, name="X"):
    return c(name, 128 * (2 * s + d), 128 * (2 * s + d) + 128)


def lists_of_w(p, t):
    pa = t & 1
    v = 48 * pa
    src = c("GV", 512 * pa + 16 * t, 512 * pa + 16 * t + 16)
    ts(p, c("uh", 0, 16), src, 0.125, OP.mult, 1536 + 160 - 0.4375, OP.add)
    ts(p, c("hh", 0, 16), src, 1.0 / 128, OP.mult, 1536 + 10 - 63.5 / 128, OP.add)
    ts(p, c("vuL", v + 16, v + 32), c("uh", 0, 16), -1536.0, OP.add)
    ts(p, c("vuL", v + 32, v + 48), c("uh", 0, 16), NU - 1536.0, OP.add)
    ts(p, c("hl", 0, 16), c("hh", 0, 16), -1536.0, OP.add, col(C20), OP.add)
    ts(p, c("wuF", 32 * pa, 32 * pa + 16), src, float(CEN), OP.add)
    ts(p, c("wuF", 32 * pa + 16, 32 * pa + 32), c("uh", 0, 16), -1536.0, OP.add)


def first_lanes(p, t):
    v = 48 * (t & 1)
    act(p, c("G12", 0, 512), c("T12", 0, 640), AF.Copy, offs=c("vuL", v + 16, v + 48), tag="G12")
    for h in (0, 1):
        mm(p, c("b5", 0, 128), c("G12", 128 * h, 128 * h + 128), c("Ib", 0, 128), True, True)
        mm(p, c("b5", 128, 288), c("G12", 256 + 128 * h, 256 + 128 * h + 128), c("R2", 0, 160), True, True)
        act(p, c("LOH", 288 * h, 288 * h + 288), c("b5", 0, 288), AF.Relu, scale=c("swt", h, h + 1))
    for h in (0, 1):
        mm(p, c("b5", 288, 448), c("LOH", 288 * h, 288 * h + 128), c("LOH", 288 * h + 128, 288 * h + 288), h == 0, h == 1)
    act(p, c("Fs", 0, 160), c("b5", 288, 448), AF.Copy)
    gtt(p, c("Pf", 0, 256), c("Fs", 0, 160), c("hl", 0, 16), c("G12", 0, 256), OP.mult, tag="Pf")
    for r in range(16):
        mm(p, c("b5", 448, 464), c("W", 15 - r, 143 - r), c("Pf", r, 256, 16), r == 0, r == 15)
    tt(p, c("M2", 0, 16), c("b5", 448, 464), c("THR", 0, 16), OP.is_gt, tag="nf")


def turn(p, out, lo, k, lo2=0, n=128, start=True, name="X"):
    for ql in (0, 1):
        for par in (0, 1):
            mm(p, c(out, lo + ql, lo + 2 * n, 2), X(ql, par, name), c("TRK", k + 128 * par + lo2, k + 128 * par + lo2 + n), start and par == 0, par == 1 and (ql == 1 or start))


def canal_lists(p, t):
    pa = t & 1
    gcp(p, c("KN", 0, 512), c("can", 0, NU), c("vuL", 48 * pa, 48 * pa + 32), tag="KN")
    for ty in (0, 1):
        for b in range(8):
            k = 512 * pa + 256 * ty
            vtr(p, c("TRK", k + b, k + 256, 8), c("KN", 256 * ty + 32 * b, 256 * ty + 32 * b + 32), tag="trk")
    turn(p, "b3", 0, 512 * pa)
    ts(p, c("KL", 0, 256), c("b3", 0, 256), float(CEN), OP.add, tag="KL")


def to_rows(p, src, lo):
    for par in (0, 1):
        for h in (0, 1):
            for ql in (0, 1):
                a, o = lo + 256 * h, 256 + 128 * par + 64 * h
                mm(p, c("b3", o, o + 64), X(par, ql), c(src, a + ql, a + 128, 2), ql == 0, ql == 1)
    for b in range(8):
        vtr(p, c("VN", 32 * b, 32 * b + 32), c("b3", 256 + b, 512, 8), tag="trv")


def sums(p, bank, o, src, a, stop=True):
    for r in range(16):
        mm(p, c(bank, o, o + 64), c("W", 15 - r, 143 - r), c(src, a + r, a + 1024, 16), r == 0, r == 15 and stop)


def trail_chunk(p, t, j):
    pa = t & 1
    a, e = 1024 * j, 1024 * j + 1024
    offs = c("GL", 256 * pa + 64 * j, 256 * pa + 64 * j + 64)
    if j in BY_ACT:
        act(p, c("R", a, e), c("xs", 0, NC), AF.Copy, offs=offs, tag="R%d" % j)
        for k in (0, 1):
            bank = "b6" if k == 0 else "b7"
            mm(p, c(bank, 0, 512), c("Ib", 0, 128), c("R", a + 512 * k, a + 512 * k + 512), True, False)
            mm(p, c(bank, 0, 512), c("Im1", 0, 128), c("zr", 1024 * pa, 1024 * pa + 512), False, True)
            act(p, c("AB", a + 512 * k, a + 512 * k + 512), c(bank, 0, 512), AF.Abs, tag="abs")
    else:
        gtt(p, c("D", a, e), c("xs", 0, NC), offs, c("zr", 1024 * pa, 1024 * pa + 1024), OP.subtract, tag="A%d" % j)
        act(p, c("AB", a, e), c("D", a, e), AF.Abs, tag="abs")
    act(p, c("SG", a, e), c("AB", a, e), AF.Sign, bias=c("lc", pa, pa + 1), tag="sign")
    sums(p, "b0" if j < 2 else "b1", 64 * (j & 1), "SG", a)


def score_chunk(p, t, j):
    pa = t & 1
    gtt(p, c("E", 1024 * j, 1024 * j + 1024), c("xs", 0, NC), c("KL", 64 * j, 64 * j + 64), c("zr", 1024 * pa, 1024 * pa + 1024), OP.max, tag="B%d" % j)
    sums(p, "b2", 64 * j, "E", 1024 * j, False)
    turn(p, "b2", 64 * j, 512 * pa, 32 * j, 32, False, "Xs")


def blend(p, t, h):
    pa, nx = t & 1, 1 - (t & 1)
    bank, s = "b%d" % h, 128 * h
    act(p, c("SM", s, s + 128), c(bank, 0, 128), AF.Relu, tag="SM")
    act(p, c("NM", s, s + 128), c(bank, 0, 128), AF.Relu, bias=2.0, scale=-1.0)
    g0, g1 = 512 * pa + 256 * h, 512 * nx + 256 * h
    for ty in (0, 1):
        o = 128 * ty
        mm(p, c("b4", o, o + 128), c("Ih", 0, 128), c("GV", g0, g0 + 128), True, False)
        mm(p, c("b4", o, o + 128), c("Ineg", 0, 128), c("SM", s, s + 128), False, True)
        mm(p, c("b4", o + 256, o + 384), c("Ineg", 0, 128), c("NM", s, s + 128), True, False)
        turn(p, "b4", o + 256, 512 * pa + 256 * ty, 64 * h, 64, False)
    act(p, c("BS", 256 * h, 256 * h + 256), c("b4", 256, 512), AF.Copy)
    tt(p, c("GV", g1, g1 + 256), c("b4", 0, 256), c("BS", 256 * h, 256 * h + 256), OP.max, tag="blend")
    ts(p, c("GL", 256 * nx + s, 256 * nx + s + 128), c("GV", g1, g1 + 128), float(CEN), OP.add, tag="GL")


def replay_value(p, t):
    pa = t & 1
    raw = t // 4 in BY_ACT
    d = c("R" if raw else "D", 256 * t, 256 * t + 256)
    z, I = c("zr", 1024 * pa, 1024 * pa + 256), c("Ib", 0, 128)
    n = c(BK["skip"], 0, 256)
    mm(p, n, c("BD", 0, 128), c("SG", 256 * t, 256 * t + 256), True, True)
    act(p, c("SW", 0, 256), n, AF.Relu)
    act(p, c("NW", 0, 256), n, AF.Relu, bias=2.0, scale=-1.0)
    lo, hi = c("b7", 0, 256), c("b7", 256, 512)
    mm(p, lo, c("Ihalf", 0, 128), d, True, False)
    mm(p, lo, c("Ihalf", 0, 128) if raw else I, z, False, False)
    mm(p, lo, c("Ineg", 0, 128), c("SW", 0, 256), False, True)
    mm(p, hi, I, d, True, False)
    if not raw:
        mm(p, hi, I, z, False, False)
    mm(p, hi, I, c("four", 0, 256), False, False)
    mm(p, hi, c("Ineg", 0, 128), c("NW", 0, 256), False, True)
    act(p, c("PB", 0, 256), lo, AF.Identity, bias=-0.25)
    tt(p, c("XM", 0, 256), hi, c("PB", 0, 256), OP.max, tag="xm")
    ts(p, c("XW", 0, 256), c("XM", 0, 256), 191.0, OP.min)


def write_lists(p, t):
    pa = t & 1
    ts(p, c("skb", 0, 16), c("SM", 16 * t, 16 * t + 16), 0.5, OP.is_gt)
    if t < STEPS - 1:
        mm(p, c("b5", 464, 480), c("one", 0, 128), c("skb", 0, 16), True, True)
        act(p, c("ssj", 0, 16), c("b5", 464, 480), AF.Copy, accum=c("sc", 0, 1))
        cp(p, c("scI", 0, 1), c("sc", 0, 1))
        ts(p, c("sdI", 0, 1), c("scI", 0, 1), 3, OP.bitwise_and)
        ts(p, c("lc", 1 - pa, 2 - pa), c("sdI", 0, 1), -1.0, OP.mult, -16.5, OP.add)
    tt(p, c("M2", 16, 32), c("M2", 0, 16), c("skb", 0, 16), OP.max)
    tt(p, c("M3", 0, 32), c("M2", 0, 32), c("DUMP", 0, 32), OP.mult)
    tt(p, c("M4", 0, 32), c("M3", 0, 32), c("wuF", 32 * pa, 32 * pa + 32), OP.max)
    cp(p, c("wcl", 0, 32), c("M4", 0, 32))


def cut_choice(p, t):
    nx = 1 - (t & 1)
    act(p, c("kS", 0, 128), c("b2", 128, 256), AF.Copy)
    tt(p, c("k1", 0, 128), c("b2", 0, 128), c("kS", 0, 128), OP.max, tag="k1")
    tt(p, c("k2", 0, 64), c("k1", 0, 64), c("k1", 64, 128), OP.max)
    tt(p, c("k3", 0, 32), c("k2", 0, 32), c("k2", 32, 64), OP.max)
    tt(p, c("km", 0, 16), c("k3", 0, 16), c("k3", 16, 32), OP.max)
    cp(p, c("kr", 0, 16), c("km", 0, 16))
    tt(p, c("kd", 0, 16), c("kr", 0, 16), c("km", 0, 16), OP.subtract)
    ts(p, c("cl", 0, 16), c("kd", 0, 16), 4096.0, OP.mult, float(CEN), OP.add, tag="cl")
    ts(p, c("c16", 0, 16), c("kd", 0, 16), 4096.0, OP.mult)
    act(p, c("cF", 0, 16), c("kd", 0, 16), AF.Identity, bias=float(CEN), scale=4096.0)
    if t < STEPS - 1:
        ts(p, c("vh", 0, 16), c("kd", 0, 16), 512.0, OP.mult, 1536 + 160 - 0.4375, OP.add)
        ts(p, c("vuL", 48 * nx, 48 * nx + 16), c("vh", 0, 16), -1536.0, OP.add)


def gauge(p, t):
    pa = t & 1
    act(p, c("xc", 0, 256), c("xs", 0, NC), AF.Copy, offs=c("cl", 0, 16), tag="xc")
    if t < STEPS - 1:
        zt, n = c("zn", 256 * t, 256 * t + 256), c(BK["zn"], 128, 384)
        mm(p, n, c("Ib", 0, 128), c("xc", 0, 256), True, False)
        mm(p, n, c("Ib", 0, 128), c("zr", 1024 * pa, 1024 * pa + 256), False, True)
        act(p, zt, n, AF.Identity, bias=-0.25, scale=0.5, tag="zn")
        add(p, "g", ("send", t), [zt], [], 0.1)
        add(p, "net", ("net", t), [zt], [c("zland", 256 * t, 256 * t + 256)], NET)
        for k in range(4):
            o = 1024 * (1 - pa) + 256 * k
            i = cp(p, c("zr", o, o + 256), c("zland", 256 * t, 256 * t + 256), tag="zr")
            p["ops"][i]["ext"] = t
    act(p, c("xh", 0, 256), c("xc", 0, 256), AF.Identity, bias=63.75, scale=0.5)


def cut_lists(p, t):
    bk = BK["dup"]
    mm(p, c(bk, 128, 368), c("Ib", 0, 128), c("TRI", 0, 240), True, False)
    for s in range(1, 16):
        o = 128 + 16 * (s - 1)
        mm(p, c(bk, o, o + 16), c("Y", 16 - s, 144 - s), c("c16", 0, 16), False, False)
        mm(p, c(bk, o, o + 16), c("Imh", 0, 128), c("c16", 0, 16), False, s == 15)
    ts(p, c("EQ", 0, 240), c(bk, 128, 368), 0.0, OP.is_equal, tag="EQ")
    for s in range(15):
        mm(p, c(bk, 368, 384), c("Ib", 0, 128), c("EQ", 16 * s, 16 * s + 16), s == 0, s == 14)
    ts(p, c("dd", 0, 16), c(bk, 368, 384), 0.5, OP.is_gt, col(DC), OP.mult)
    tt(p, c("cdI", 0, 16), c("dd", 0, 16), c("cF", 0, 16), OP.max)
    cp(p, c("cdl", 0, 32, 2), c("cdI", 0, 16))


def step(p, t):
    pa, nx = t & 1, 1 - (t & 1)
    na = nb = 0
    for ch in ORDER:
        if ch == "A":
            trail_chunk(p, t, na)
            na += 1
            if na == 2:
                blend(p, t, 0)
                replay_value(p, t)
                write_lists(p, t)
            if na == 4:
                blend(p, t, 1)
        else:
            score_chunk(p, t, nb)
            nb += 1
            if nb == 4:
                cut_choice(p, t)
                gauge(p, t)
                cut_lists(p, t)
    k = t + 3
    g1 = 512 * nx + 256 * (k // 8) + 16 * (k % 8)
    cp(p, c("GV", g1, g1 + 16), c("c16", 0, 16))
    cp(p, c("GL", 256 * nx + 16 * k, 256 * nx + 16 * k + 16), c("cl", 0, 16))
    scat(p, c("xs", 0, NC + B), c("wcl", 0, 16), c("XW", 0, 256), tag="scw")
    for q in range(16):
        scat(p, c("xs", 0, NC + B), c("cdl", 2 * q, 2 * q + 1), c("xh", 16 * q, 16 * q + 16), tag="scc")
    to_rows(p, "GV", 512 * nx + 128)
    scat(p, c("can", 0, NU + B), c("wcl", 16, 32), c("VN", 0, 256), tag="sccan")
    if t < STEPS - 1:
        lists_of_w(p, t + 1)
        first_lanes(p, t + 1)
        canal_lists(p, t + 1)


def prologue(p):
    dma(p, c("trI", 0, 256), "trail", 0)
    dma(p, c("canI", 0, 320), "canal", 1)
    dma(p, ("cutI", 0, 256, 1, 8), "cut", 2)
    dma(p, c("zraw", 0, 256), "z", 3)
    dma(p, c("xraw", 0, NC), "x", 4)
    constants(p)
    ts(p, c("tr16", 0, 256), c("trI", 0, 256), -float(CEN), OP.add)
    mm(p, c("b7", 0, 256), c("PS", 0, 128), c("tr16", 0, 256), True, True)
    cp(p, c("KN", 0, 256), c("b7", 0, 256))
    for b in range(8):
        vtr(p, c("TRK", 512 + b, 512 + 256, 8), c("KN", 32 * b, 32 * b + 32))
    turn(p, "b3", 0, 512)
    ts(p, c("GL", 0, 256), c("b3", 0, 256), float(CEN), OP.add)
    for h in (0, 1):
        cp(p, c("GV", 256 * h, 256 * h + 128), c("b3", 128 * h, 128 * h + 128))
    ts(p, ("cut16", 0, 256, 1, 8), ("cutI", 0, 256, 1, 8), -float(CEN), OP.add)
    for r in range(16):
        mm(p, c("b6", 0, 16), ("ZW", 15 - r, 143 - r, 1, 8), ("cut16", r, 256, 16, 8), r == 0, r == 15)
    ts(p, c("vh", 0, 16), c("b6", 0, 16), 0.125, OP.mult, 1536 + 160 - 0.4375, OP.add)
    ts(p, c("vuL", 0, 16), c("vh", 0, 16), -1536.0, OP.add)
    ts(p, c("can16", 0, 320), c("canI", 0, 320), -float(CEN), OP.add)
    mm(p, c("b4", 0, 320), c("PS", 0, 128), c("can16", 0, 320), True, True)
    act(p, c("can", 0, 320), c("b4", 0, 320), AF.Copy)
    lists_of_w(p, 0)
    first_lanes(p, 0)
    canal_lists(p, 0)
    for k in range(4):
        act(p, c("zr", 256 * k, 256 * k + 256), c("zraw", 0, 256), AF.Identity, bias=128.0)
    act(p, c("xs", 0, NC), c("xraw", 0, NC), AF.Identity, bias=128.0)


def epilogue(p):
    cp(p, c("can16", 0, 320), c("can", 0, 320))
    mm(p, c("b4", 0, 320), c("PS", 128, 256), c("can16", 0, 320), True, True)
    act(p, c("outF", 0, 320), c("b4", 0, 320), AF.Identity, bias=float(CEN))
    dma(p, "yl", c("outF", 0, 320), 5)
    to_rows(p, "GV", 0)
    cp(p, c("trO", 0, 256), c("VN", 0, 256))
    mm(p, c("b7", 0, 256), c("PS", 128, 256), c("trO", 0, 256), True, True)
    act(p, c("outG", 0, 256), c("b7", 0, 256), AF.Identity, bias=float(CEN))
    dma(p, "yg", c("outG", 0, 256), 6)
    h = NC // 2
    ts(p, c("xo", 0, h), c("xs", 0, h), -128.0, OP.add)
    dma(p, "yx", c("xo", 0, h), 7, 0, h)
    act(p, c("xo", h, NC), c("xs", h, NC), AF.Identity, bias=-128.0)
    dma(p, "yx", c("xo", h, NC), 8, h, NC)


LONG = ("A0", "A1", "A2", "A3", "B0", "B1", "B2", "B3")


def schedule(p):
    ops = p["ops"]
    n = len(ops)
    succ = [[] for _ in range(n)]
    for i in range(n):
        for j in ops[i]["deps"]:
            succ[j].append(i)
    tail = [0.0] * n
    for i in range(n - 1, -1, -1):
        tail[i] = ops[i]["cost"] + max([tail[k] + (0.0 if ops[k]["q"] == ops[i]["q"] else 0.06) for k in succ[i]] or [0.0])
    left = [len(o["deps"]) for o in ops]
    ready = [0.0] * n
    pools = {"v": [], "a": [], "p": [], "g": [], "sync": [], "net": []}
    free = {q: 0.0 for q in pools}
    order = {q: [] for q in pools}
    for i in range(n):
        if left[i] == 0:
            pools[ops[i]["q"]].append(i)
    p["span"] = 0.0
    for _ in range(n):
        t0, q = min((max(free[q], min(ready[i] for i in pools[q])), q) for q in pools if pools[q])
        cand = [i for i in pools[q] if ready[i] <= t0 + 1e-9]
        if q == "v":
            few = [k for k in cand if ops[k]["tag"] not in LONG]
            i = max(few, key=lambda k: (tail[k], -k)) if few else min(cand)
        elif q == "a":
            few = [k for k in cand if ops[k]["cost"] < SMALL] or cand
            i = max(few, key=lambda k: (tail[k], -k))
        else:
            i = max(cand, key=lambda k: (tail[k], -k))
        pools[q].remove(i)
        fin = t0 + ops[i]["cost"]
        free[q] = t0 if q == "net" else t0 + 0.1 if q == "sync" else fin
        p["span"] = max(p["span"], fin)
        order[q].append(i)
        for k in succ[i]:
            ready[k] = max(ready[k], fin + (0.06 if ops[k]["q"] != q else 0.0 if q == "p" else 0.03))
            left[k] -= 1
            if left[k] == 0:
                pools[ops[k]["q"]].append(k)
    p["order"] = order
    seq, ptr, out = [], {q: 0 for q in order}, set()
    while len(seq) < n:
        for q in order:
            while ptr[q] < len(order[q]) and all(j in out for j in ops[order[q][ptr[q]]]["deps"]):
                seq.append(order[q][ptr[q]])
                out.add(order[q][ptr[q]])
                ptr[q] += 1
    p["emit"] = seq


_CACHE = {}


def program():
    if "p" not in _CACHE:
        p = {"ops": [], "acc": {}, "bank": {}}
        prologue(p)
        for t in range(STEPS):
            step(p, t)
        epilogue(p)
        schedule(p)
        _CACHE["p"] = p
    return _CACHE["p"]


SEMOF = {"v": "sv", "a": "sa", "p": "sp", "g": "sg"}


def dest(T, r, t):
    return T.cores[(r + 1 + t % 7) % len(T.cores)]


def relay_of(topo, T, src, dst):
    if topo.may_write(src, dst):
        return None
    cand = [k for k in topo.cores_of(src) if T.rank_of(k) is None and topo.may_write(k, dst)]
    same = [k for k in cand if topo.die(k) == topo.die(src)]
    return (same or cand)[0]


def hand_on(g, core, T, topo):
    sent = 0
    for t in range(STEPS - 1):
        for r in range(len(T.cores)):
            src, dst = T.cores[r], dest(T, r, t)
            if core in topo.cores_of(src) and relay_of(topo, T, src, dst) == core:
                g.wait_ge(T.sem["r%d" % t], len(topo.engines(src, core)))
                rid, pid = topo.addr(dst, core)
                g.remote_dma(T.zland[:, 256 * t:256 * t + 256], T.relay[:, 256 * t:256 * t + 256], T.sem["z%d" % t], T.sem.zl, pid, rid, topo.mask(core, dst))
                sent += len(topo.engines(core, dst))
    if sent:
        g.wait_ge(T.sem.zl, sent)


def rank_program(g, core, T, topo):
    rank = T.rank_of(core)
    if rank is None:
        hand_on(g, core, T, topo)
        return
    p = program()
    ops = p["ops"]
    queue = {"v": g.vector, "a": g.scalar, "p": g.tensor, "g": g, "sync": g.sync}
    known = {q: {} for q in queue}
    clk, gpos, seen = {}, {}, {}
    count = {"v": 0, "a": 0, "p": 0, "g": 0}
    sent = 0
    for i in p["emit"]:
        o = ops[i]
        q = o["q"]
        if q == "net":
            continue
        kn, need = known[q], {}
        for j, w in o["deps"].items():
            oj = ops[j]
            if oj["q"] == "net" or not w or isinstance(oj["fn"], tuple):
                continue
            s, v = (oj["dsem"], 16) if oj["dsem"] else (SEMOF[oj["q"]], gpos[j])
            if kn.get(s, 0) < v and need.get(s, (0, 0))[0] < v:
                need[s] = (v, j)
        for s in list(need):
            if any(s2 != s and clk[need[s2][1]].get(s, 0) >= need[s][0] for s2 in need):
                del need[s]
        for s, (v, j) in need.items():
            queue[q].wait_ge(T.sem[s], v)
            for s2, v2 in clk[j].items():
                kn[s2] = max(kn.get(s2, 0), v2)
        t = o["ext"]
        if t is not None and (q, t) not in seen:
            seen[(q, t)] = True
            for src in T.cores:
                if dest(T, T.rank_of(src), t) == core:
                    via = relay_of(topo, T, src, core)
                    queue[q].wait_ge(T.sem["z%d" % t], len(topo.engines(src if via is None else via, core)))
        if isinstance(o["fn"], tuple):
            t = o["fn"][1]
            dst = dest(T, rank, t)
            via = relay_of(topo, T, core, dst)
            to = dst if via is None else via
            rid, pid = topo.addr(to, core)
            g.remote_dma((T.zland if via is None else T.relay)[:, 256 * t:256 * t + 256], T.zn[:, 256 * t:256 * t + 256],
                         T.sem[("z%d" if via is None else "r%d") % t], T.sem.zl, pid, rid, topo.mask(core, to))
            sent += len(topo.engines(core, to))
            continue
        ins = o["fn"](g, T)
        clk[i] = dict(kn)
        if o["dsem"]:
            ins.then_inc(T.sem[o["dsem"]], 16)
            clk[i][o["dsem"]] = 16
        else:
            ins.then_inc(T.sem[SEMOF[q]], 1)
            count[q] += 1
            gpos[i] = clk[i][SEMOF[q]] = count[q]
    for q in count:
        g.wait_ge(T.sem[SEMOF[q]], count[q])
    for o in ops:
        if o["dsem"]:
            g.wait_ge(T.sem[o["dsem"]], 16)
    g.wait_ge(T.sem.zl, sent)
